import numpy as np
import ml_dtypes


def mxq(x, axis, fmt="e4m3"):
    dtype, down = {"e4m3": (ml_dtypes.float8_e4m3fn, 7), "e5m2": (ml_dtypes.float8_e5m2, 14)}[fmt]
    v = np.moveaxis(np.asarray(x, np.float32).astype(ml_dtypes.bfloat16).astype(np.float64), axis, -1)
    blocks = v.reshape(v.shape[:-1] + (-1, 32))
    amax = np.abs(blocks).max(-1, keepdims=True)
    byte = np.maximum(np.where(amax > 0, np.frexp(amax)[1] - 1 + 127, 0) - down, 1)
    scale = np.exp2(byte - 127.0)
    codes = (blocks / scale).astype(np.float32).astype(dtype).astype(np.float64)
    return np.moveaxis((codes * scale).reshape(v.shape), -1, axis)


WIDE = False


def mx_kscale(k):
    if not WIDE:
        return np.ones(k)
    levels = np.array([10, -10, 5, -5, 0])
    if k % 512:
        return np.exp2(np.random.permutation(np.resize(levels, k // 32))).repeat(32)
    a = np.empty((k // 512, 16))
    for p in range(k // 512):
        a[p, :8] = np.random.permutation(np.resize(levels, 8))
        for g in range(8):
            far = levels[np.abs(levels - a[p, g]) >= 10]
            a[p, g + 8] = far[np.random.randint(len(far))]
    return np.exp2(a.ravel()).repeat(32)


BF16 = ml_dtypes.bfloat16


def bf(x):
    return np.asarray(x, np.float32).astype(BF16)


def f64(x):
    return np.asarray(x).astype(np.float64)


E2M1 = np.array([0.0, 0.5, 1.0, 1.5, 2.0, 3.0, 4.0, 6.0, -0.0, -0.5, -1.0, -1.5, -2.0, -3.0, -4.0, -6.0])


def pack_weight(w, fmt):
    k, n = w.shape
    w = f64(bf(w)).reshape(k // 32, 32, n)
    amax = np.abs(w).max(1)
    if fmt == "e4m3":
        byte = np.frexp(amax)[1] - 1 + 127 - 7
    else:
        mant, ex = np.frexp(amax / 6.0)
        byte = np.where(mant > 0.5, ex, ex - 1) + 127
    byte = np.clip(np.where(amax > 0, byte, 1), 1, 254)
    scaled = (w * np.exp2(127.0 - byte)[:, None, :]).reshape(k, n).astype(np.float32)
    by_word = np.ascontiguousarray(scaled.reshape(k // 512, 128, 4, n).transpose(0, 1, 3, 2))
    if fmt == "e4m3":
        words = by_word.astype(ml_dtypes.float8_e4m3fn).view(np.uint8)
    else:
        c = by_word.astype(ml_dtypes.float4_e2m1fn).view(np.uint8) & 0xF
        words = c[..., 0::2] | (c[..., 1::2] << 4)
    return np.ascontiguousarray(words), np.ascontiguousarray(byte.astype(np.uint8).reshape(k // 512, 16, n))


def unpack_weight(words, scales, fmt):
    g, p, n, _ = words.shape
    if fmt == "e4m3":
        vals = np.ascontiguousarray(words).view(ml_dtypes.float8_e4m3fn).astype(np.float64)
    else:
        nib = np.empty((g, p, n, 4), np.uint8)
        nib[..., 0::2] = words & 0xF
        nib[..., 1::2] = words >> 4
        vals = E2M1[nib]
    vals = vals * np.repeat(np.exp2(scales.astype(np.float64) - 127.0), 8, axis=1)[..., None]
    return vals.transpose(0, 1, 3, 2).reshape(g * 512, n)
def pack4(w):
    words, scales = pack_weight(w, "e2m1")
    return words.reshape(words.shape[0], 128, -1), scales


def unpack4(words, scales):
    return unpack_weight(words.reshape(words.shape[0], 128, -1, 2), scales, "e2m1")


G, M, O, F, R = 4, 1024, 512, 1024, 512


def setup_inputs():
    so, u = mx_kscale(G * O), mx_kscale(M)
    wt = np.random.standard_normal((G * O, F)) / np.sqrt(O) / so[:, None]
    wt_words, wt_scales = pack4(wt)
    c = np.random.standard_normal((M, R))
    c[:, 0] = 1
    return {"e": bf(np.random.standard_normal((G, M, O)) * so.reshape(G, 1, O) * u[:, None]),
            "wt_words": wt_words,
            "wt_scales": wt_scales,
            "v": bf(np.random.standard_normal((G, M, F)) - 0.25),
            "beta": bf(1 + 0.1 * np.random.standard_normal((G, F))),
            "c": bf(c / np.sqrt(M) / u[:, None])}


def reference(e, wt_words, wt_scales, v, beta, c):
    e, v, beta = f64(e), f64(v), f64(beta)
    wt = unpack4(wt_words, wt_scales)
    cq = mxq(f64(c), 0, "e4m3")
    grads = []
    for j in range(G):
        d = mxq(e[j], 1, "e4m3") @ wt[j * O:(j + 1) * O]
        z = d * (v[j] >= 0) * beta[j]
        grads.append(cq.T @ mxq(z, 0, "e4m3"))
    return np.stack(grads)

@@ -1,0 +1,353 @@
+from contextlib import ExitStack
+
+import concourse.mybir as mybir
+from concourse.masks import make_identity
+
+G, M, O, F, R = 4, 1024, 512, 1024, 512
+FLOPS = 2 * G * M * O * F + 2 * G * M * F * R
+
+F32 = mybir.dt.float32
+BF16 = mybir.dt.bfloat16
+U32 = mybir.dt.uint32
+I32 = mybir.dt.int32
+U8 = mybir.dt.uint8
+FP8 = mybir.dt.float8_e4m3fn_x4
+FP4 = mybir.dt.float4_e2m1fn_x4
+ALU = mybir.AluOpType
+ACT = mybir.ActivationFunctionType
+
+P = 128
+N_SLOT = 16
+NB = [2, 3, 3] + [2] * 9 + [3, 3, 3, 0]
+
+
+def tile_pact_threshold_grad_s14_kernel(tc, e, wt_words, wt_scales, v, beta, c, out):
+    nc = tc.nc
+    with ExitStack() as ctx:
+        keep = ctx.enter_context(tc.tile_pool(name="keep", bufs=1))
+        work = ctx.enter_context(tc.tile_pool(name="work", bufs=2))
+        psum = ctx.enter_context(tc.psum_pool(name="psum", bufs=2))
+        ctx.enter_context(tc.manual_schedule())
+
+        def slot_of(k):
+            return k // 4, (k % 4) // 2, k % 2
+
+        planes = keep.tile([P, G * F], U8, align_bytes=64, name="planes")
+        nc.vector.memset(planes[:].bitcast(I32), 0)
+        brow = keep.tile([P, P], BF16, align_bytes=64, name="brow")
+        nc.vector.memset(brow[:], 0.0)
+        warm = keep.tile([P, 2], F32, name="warm")
+        nc.vector.memset(warm[:], 0.0)
+        ident_b = keep.tile([P, P], BF16, align_bytes=64, name="ident_b")
+        make_identity(nc, ident_b[:])
+        ident_f = keep.tile([P, P], F32, align_bytes=64, name="ident_f")
+        make_identity(nc, ident_f[:])
+
+        nc.scalar.dma_start(out=brow[0:32, :], in_=beta.rearrange("j (b f) -> (j b) f", f=P))
+        for quad in range(4):
+            nc.scalar.dma_start(
+                out=planes[32 * quad : 32 * quad + 4, :].bitcast(I32).rearrange("r (j n) -> r j n", j=G),
+                in_=wt_scales[:, 4 * quad : 4 * quad + 4, :].bitcast(I32).rearrange("j r n -> r j n"),
+            )
+        nc.scalar.activation(out=warm[:, 1:2], in_=warm[:, 0:1], func=ACT.Copy, scale=1.0)
+
+        e_sb, v_sb, w_sb, e_codes, e_scales, betab = {}, {}, {}, {}, {}, {}
+        for n in range(8):
+            e_sb[n] = keep.tile([P, 4 * O], BF16, align_bytes=64, name="e_sb%d" % n)
+            v_sb[n] = keep.tile([P, 4, F], BF16, align_bytes=64, name="v_sb%d" % n)
+            e_codes[n] = keep.tile([P, 512], U32, align_bytes=64, name="e_codes%d" % n)
+            e_scales[n] = keep.tile([P, 512], U8, align_bytes=64, name="e_scales%d" % n)
+        for j in range(G):
+            w_sb[j] = keep.tile([P, 2 * F], U8, align_bytes=64, name="w_sb%d" % j)
+            betab[j] = keep.tile([P, F], BF16, align_bytes=64, name="betab%d" % j)
+        c_sb = keep.tile([P, 2, 4, R], BF16, align_bytes=64, name="c_sb")
+
+        def load_e(n):
+            j, g = n // 2, n % 2
+            nc.sync.dma_start(
+                out=e_sb[n][:].rearrange("p (t k) -> p t k", t=4),
+                in_=e[j, 512 * g : 512 * g + 512, :].rearrange("(p t) k -> p t k", t=4),
+            )
+
+        def load_v(n, lo, hi):
+            j, g = n // 2, n % 2
+            nc.sync.dma_start(
+                out=v_sb[n][:, :, lo:hi],
+                in_=v[j, 512 * g : 512 * g + 512, lo:hi].rearrange("(p t) f -> p t f", t=4),
+            )
+
+        def load_w(j):
+            nc.sync.dma_start(out=w_sb[j][:].bitcast(I32), in_=wt_words[j].bitcast(I32))
+
+        load_e(0)
+        load_v(0, 0, 512)
+        load_w(0)
+        load_e(1)
+        load_v(1, 0, 512)
+        load_v(0, 512, 1024)
+        load_v(1, 512, 1024)
+        for g in range(2):
+            nc.sync.dma_start(
+                out=c_sb[:, g, :, :],
+                in_=c[512 * g : 512 * g + 512, :].rearrange("(p t) r -> p t r", t=4),
+            )
+        for j in range(1, G):
+            load_e(2 * j)
+            load_w(j)
+            load_e(2 * j + 1)
+            load_v(2 * j, 0, F)
+            load_v(2 * j + 1, 0, F)
+
+        e_grp = {}
+
+        def e_transpose(n, half):
+            if half == 0:
+                eg = work.tile([P, 2048], BF16, align_bytes=64, name="eg")
+                e_grp[n] = eg
+            et = psum.tile([P, 2, 2, P], F32, bufs=1, name="et")
+            words = e_sb[n][:].bitcast(F32)
+            for tt in range(2):
+                for u in range(2):
+                    lo = 256 * (2 * half + tt)
+                    nc.tensor.transpose(et[:, tt, u, :], words[:, lo + u : lo + 256 : 2], ident_f[:])
+            return et
+
+        def e_copy(n, half, et, on_vector=False):
+            dst = e_grp[n][:, 1024 * half : 1024 * half + 1024].bitcast(F32)
+            dst = dst.rearrange("p (t m u) -> p t m u", t=2, u=2)
+            src = et[:].rearrange("p t u m -> p t m u")
+            if on_vector:
+                nc.vector.tensor_copy(out=dst, in_=src)
+            else:
+                nc.scalar.copy(out=dst, in_=src)
+
+        def e_quant(n):
+            nc.vector.quantize_mx(out=e_codes[n][:].bitcast(FP8), scales=e_scales[n][:], in_=e_grp[n][:])
+
+        def a_blocks(k):
+            return list(range(4 - NB[k])) if 0 <= k < N_SLOT else []
+
+        def b_blocks(k):
+            return list(range(4 - NB[k], 4)) if 0 <= k < N_SLOT else []
+
+        bcol_b = keep.tile([P, 32], BF16, name="bcol_b")
+        bcol_f = keep.tile([P, 32], F32, name="bcol_f")
+
+        def beta_columns():
+            yt = psum.tile([P, 4, P], BF16, name="yt")
+            nc.tensor.transpose(yt[:, 0, :], brow[:], ident_b[:])
+            nc.scalar.copy(out=bcol_b[:], in_=yt[:, 0, 0:32])
+            nc.vector.tensor_copy(out=bcol_f[:], in_=yt[:, 0, 0:32])
+
+        def beta_rows(j):
+            for q in range(2):
+                count = max(len(a_blocks(4 * j + 2 * q)), len(a_blocks(4 * j + 2 * q + 1)))
+                if count:
+                    yt = psum.tile([P, 4, P], BF16, name="yt")
+                    for b in range(count):
+                        i = 8 * j + 4 * q + b
+                        nc.tensor.transpose(yt[:, b, :], bcol_b[:, i : i + 1].to_broadcast([P, P]), ident_b[:])
+                    nc.scalar.copy(
+                        out=betab[j][:, 512 * q : 512 * q + P * count],
+                        in_=yt[:, 0:count, :].rearrange("p b f -> p (b f)"),
+                    )
+
+        mks, mbs, zs, ys, yts = {}, {}, {}, {}, {}
+
+        def mask(k):
+            width = P * len(a_blocks(k))
+            if width:
+                j, q, g = slot_of(k)
+                mk = work.tile([P, 4, 512], BF16, align_bytes=64, bufs=1, name="mk")
+                nc.vector.tensor_scalar(
+                    out=mk[:, :, 0:width], in0=v_sb[2 * j + g][:, :, 512 * q : 512 * q + width],
+                    scalar1=0.0, scalar2=None, op0=ALU.is_ge,
+                )
+                mks[k] = mk
+
+        def mask_beta(k):
+            width = P * len(a_blocks(k))
+            if width:
+                j, q, g = slot_of(k)
+                mb = work.tile([P, 4, 512], BF16, align_bytes=64, name="mb")
+                nc.vector.tensor_tensor(
+                    out=mb[:, :, 0:width], in0=mks[k][:, :, 0:width],
+                    in1=betab[j][:, 512 * q : 512 * q + width].unsqueeze(1).to_broadcast([P, 4, width]),
+                    op=ALU.mult,
+                )
+                mbs[k] = mb
+
+        def open_z(k):
+            z = work.tile([P, 512, 4], BF16, align_bytes=64, bufs=3, name="z")
+            zs[k] = z
+
+        def mm_a(k, b):
+            j, q, g = slot_of(k)
+            n, fb = 2 * j + g, 4 * q + b
+            da = psum.tile([P, 4, P], F32, name="da")
+            for t in range(4):
+                cols = slice(P * t, P * t + P)
+                nc.tensor.matmul_mx(
+                    out=da[:, t, :],
+                    lhsT=e_codes[n][:, cols].bitcast(FP8), lhsT_scale=e_scales[n][:, cols],
+                    rhs=w_sb[j][:, 256 * fb : 256 * fb + 256].bitcast(FP4),
+                    rhs_scale=planes[:, F * j + P * fb : F * j + P * fb + P],
+                    start=True, stop=True,
+                )
+            return da
+
+        def gate_a(k, b, da):
+            nc.vector.tensor_tensor(
+                out=zs[k][:, P * b : P * b + P, :],
+                in0=da[:].rearrange("p t f -> p f t"),
+                in1=mbs[k][:, :, P * b : P * b + P].rearrange("p t f -> p f t"),
+                op=ALU.mult,
+            )
+
+        def mm_b(k, b):
+            j, q, g = slot_of(k)
+            n, fb = 2 * j + g, 4 * q + b
+            db = psum.tile([P, 512], F32, bufs=1, name="db")
+            nc.tensor.matmul_mx(
+                out=db[:],
+                lhsT=w_sb[j][:, 256 * fb : 256 * fb + 256].bitcast(FP4),
+                lhsT_scale=planes[:, F * j + P * fb : F * j + P * fb + P],
+                rhs=e_codes[n][:].bitcast(FP8), rhs_scale=e_scales[n][:],
+                start=True, stop=True,
+            )
+            y = work.tile([P, 512], BF16, align_bytes=64, bufs=6, name="y")
+            i = 8 * j + fb
+            nc.scalar.activation(out=y[:], in_=db[:], func=ACT.Copy, scale=bcol_f[:, i : i + 1])
+            ys[k, b] = y
+
+        def y_transpose(k, b):
+            yt = psum.tile([P, 4, P], BF16, name="yt")
+            for t in range(4):
+                nc.tensor.transpose(yt[:, t, :], ys[k, b][:, P * t : P * t + P], ident_b[:])
+            yts[k, b] = yt
+
+        def gate_b(k, b):
+            j, q, g = slot_of(k)
+            lo = 512 * q + P * b
+            nc.vector.scalar_tensor_tensor(
+                out=zs[k][:, P * b : P * b + P, :],
+                in0=v_sb[2 * j + g][:, :, lo : lo + P].rearrange("p t f -> p f t"),
+                scalar=0.0,
+                in1=yts[k, b][:].rearrange("p t f -> p f t"),
+                op0=ALU.is_ge, op1=ALU.mult,
+            )
+
+        z_codes, z_scales = {}, {}
+
+        def z_quant(k, lo=0, hi=512):
+            if lo == 0:
+                zc = work.tile([P, 512], U32, align_bytes=64, bufs=5, name="zc")
+                zp = work.tile([P, 512], U8, align_bytes=64, bufs=5, name="zp")
+                z_codes[k], z_scales[k] = zc, zp
+            nc.vector.quantize_mx(
+                out=z_codes[k][:, lo:hi].bitcast(FP8), scales=z_scales[k][:, lo:hi],
+                in_=zs[k][:, lo:hi, :].rearrange("p f t -> p (f t)"),
+            )
+
+        c_codes = keep.tile([P, 2 * R], U32, align_bytes=64, name="c_codes")
+        c_scales = keep.tile([P, 2 * R], U8, align_bytes=64, name="c_scales")
+        c_grp = keep.tile([P, 2, R, 4], BF16, align_bytes=64, name="c_grp")
+
+        def c_copy(g, half):
+            cols = slice(256 * half, 256 * half + 256)
+            nc.scalar.copy(out=c_grp[:, g, cols, :], in_=c_sb[:, g, :, cols].rearrange("p t r -> p r t"))
+
+        def c_quant():
+            nc.vector.quantize_mx(
+                out=c_codes[:].bitcast(FP8), scales=c_scales[:], in_=c_grp[:].rearrange("p g r t -> p (g r t)")
+            )
+
+        def second(pair, rt, on_vector, lo=0, hi=512):
+            j, q = pair // 2, pair % 2
+            ob = psum.tile([P, 512], F32, name="ob")
+            for g in range(2):
+                k = 2 * pair + g
+                cols = slice(R * g + P * rt, R * g + P * rt + P)
+                nc.tensor.matmul_mx(
+                    out=ob[:, lo:hi],
+                    lhsT=c_codes[:, cols].bitcast(FP8), lhsT_scale=c_scales[:, cols],
+                    rhs=z_codes[k][:, lo:hi].bitcast(FP8), rhs_scale=z_scales[k][:, lo:hi],
+                    start=(g == 0), stop=(g == 1),
+                )
+            ot = work.tile([P, 512], F32, bufs=6, name="ot")
+            if on_vector:
+                nc.vector.tensor_copy(out=ot[:, lo:hi], in_=ob[:, lo:hi])
+            else:
+                nc.scalar.copy(out=ot[:, lo:hi], in_=ob[:, lo:hi])
+            nc.sync.dma_start(
+                out=out[j, P * rt : P * rt + P, 512 * q + lo : 512 * q + hi], in_=ot[:, lo:hi]
+            )
+
+        def e_head(n, on_vector):
+            for half in range(2):
+                et = e_transpose(n, half)
+                e_copy(n, half, et, on_vector and half == 1)
+
+        e_head(0, True)
+        beta_columns()
+        beta_rows(0)
+        mask(0)
+        e_quant(0)
+        mask_beta(0)
+
+        for k in range(N_SLOT):
+            job = None
+            if k < 12:
+                job = (2 * (k // 4 + 1) + (k % 4) // 2, k % 2)
+                et = e_transpose(job[0], job[1])
+            late = b_blocks(k - 1)
+            for b in late[:2]:
+                y_transpose(k - 1, b)
+            if job:
+                e_copy(job[0], job[1], et)
+            open_z(k)
+            if k:
+                mask(k + 1)
+            groups = []
+            if 3 <= k < 15:
+                groups = [((k - 3) // 2, 2 * ((k - 3) % 2) + i) for i in range(2)]
+            if k == 15:
+                groups = [(6, rt) for rt in range(4)]
+            now_a, now_b = a_blocks(k), b_blocks(k)
+            for r in range(4):
+                if r < len(now_b):
+                    mm_b(k, now_b[r])
+                if r < len(now_a):
+                    da = mm_a(k, now_a[r])
+                if r < len(late):
+                    gate_b(k - 1, late[r])
+                    if r + 2 < len(late):
+                        y_transpose(k - 1, late[r + 2])
+                if r < len(now_a):
+                    gate_a(k, now_a[r], da)
+                if k == 15 and r == 2:
+                    z_quant(14)
+                if k == 15 and r == 3:
+                    z_quant(15, 0, 256)
+                if r < len(groups):
+                    second(groups[r][0], groups[r][1], False)
+            if k == 0:
+                e_head(1, False)
+                mask(1)
+                e_quant(1)
+            if 1 <= k < 15:
+                z_quant(k - 1)
+            if job and job[1] == 1:
+                e_quant(job[0])
+            if k in (1, 2):
+                c_copy(k - 1, 0)
+                c_copy(k - 1, 1)
+            if k == 2:
+                c_quant()
+            if k in (1, 5, 9):
+                beta_rows(k // 4 + 1)
+            mask_beta(k + 1)
+        z_quant(15, 256, 512)
+        for half in range(2):
+            for rt in range(4):
+                second(7, rt, rt % 2 == 1, 256 * half, 256 * half + 256)

@@ -18,7 +18,7 @@ ACT = mybir.ActivationFunctionType
 
 P = 128
 N_SLOT = 16
-NB = [2, 3, 3] + [2] * 9 + [3, 3, 3, 0]
+NB = [2] * 15 + [0]
 
 
 def tile_pact_threshold_grad_s14_kernel(tc, e, wt_words, wt_scales, v, beta, c, out):
@@ -32,29 +32,30 @@ def tile_pact_threshold_grad_s14_kernel(tc, e, wt_words, wt_scales, v, beta, c, 
         def slot_of(k):
             return k // 4, (k % 4) // 2, k % 2
 
-        planes = keep.tile([P, G * F], U8, align_bytes=64, name="planes")
-        nc.vector.memset(planes[:].bitcast(I32), 0)
         brow = keep.tile([P, P], BF16, align_bytes=64, name="brow")
         nc.vector.memset(brow[:], 0.0)
+        planes = keep.tile([P, G * F], U8, align_bytes=64, name="planes")
+        nc.vector.memset(planes[:].bitcast(I32), 0)
         warm = keep.tile([P, 2], F32, name="warm")
         nc.vector.memset(warm[:], 0.0)
-        ident_b = keep.tile([P, P], BF16, align_bytes=64, name="ident_b")
-        make_identity(nc, ident_b[:])
         ident_f = keep.tile([P, P], F32, align_bytes=64, name="ident_f")
         make_identity(nc, ident_f[:])
+        ident_b = keep.tile([P, P], BF16, align_bytes=64, name="ident_b")
+        make_identity(nc, ident_b[:])
 
-        nc.scalar.dma_start(out=brow[0:32, :], in_=beta.rearrange("j (b f) -> (j b) f", f=P))
-        for quad in range(4):
-            nc.scalar.dma_start(
-                out=planes[32 * quad : 32 * quad + 4, :].bitcast(I32).rearrange("r (j n) -> r j n", j=G),
-                in_=wt_scales[:, 4 * quad : 4 * quad + 4, :].bitcast(I32).rearrange("j r n -> r j n"),
-            )
         nc.scalar.activation(out=warm[:, 1:2], in_=warm[:, 0:1], func=ACT.Copy, scale=1.0)
 
         e_sb, v_sb, w_sb, e_codes, e_scales, betab = {}, {}, {}, {}, {}, {}
         for n in range(8):
             e_sb[n] = keep.tile([P, 4 * O], BF16, align_bytes=64, name="e_sb%d" % n)
-            v_sb[n] = keep.tile([P, 4, F], BF16, align_bytes=64, name="v_sb%d" % n)
+            if n < 2:
+                for q in range(2):
+                    v_sb[n, q] = keep.tile([P, 4, 512], BF16, align_bytes=64, name="v_sb%d_%d" % (n, q))
+            else:
+                v_full = keep.tile([P, 4, F], BF16, align_bytes=64, name="v_sb%d" % n)
+                v_sb[n] = v_full
+                for q in range(2):
+                    v_sb[n, q] = v_full[:, :, 512 * q : 512 * q + 512]
             e_codes[n] = keep.tile([P, 512], U32, align_bytes=64, name="e_codes%d" % n)
             e_scales[n] = keep.tile([P, 512], U8, align_bytes=64, name="e_scales%d" % n)
         for j in range(G):
@@ -69,42 +70,54 @@ def tile_pact_threshold_grad_s14_kernel(tc, e, wt_words, wt_scales, v, beta, c, 
                 in_=e[j, 512 * g : 512 * g + 512, :].rearrange("(p t) k -> p t k", t=4),
             )
 
-        def load_v(n, lo, hi):
+        def load_v(n, q=None):
             j, g = n // 2, n % 2
-            nc.sync.dma_start(
-                out=v_sb[n][:, :, lo:hi],
-                in_=v[j, 512 * g : 512 * g + 512, lo:hi].rearrange("(p t) f -> p t f", t=4),
-            )
+            rows = v[j, 512 * g : 512 * g + 512, :].rearrange("(p t) f -> p t f", t=4)
+            if q is None:
+                nc.sync.dma_start(out=v_sb[n][:], in_=rows)
+            else:
+                nc.sync.dma_start(out=v_sb[n, q][:], in_=rows[:, :, 512 * q : 512 * q + 512])
 
         def load_w(j):
             nc.sync.dma_start(out=w_sb[j][:].bitcast(I32), in_=wt_words[j].bitcast(I32))
 
         load_e(0)
-        load_v(0, 0, 512)
+        nc.sync.dma_start(out=brow[0:32, :], in_=beta.rearrange("j (b f) -> (j b) f", f=P))
+        load_v(0, 0)
+        for quad in range(4):
+            nc.sync.dma_start(
+                out=planes[32 * quad : 32 * quad + 4, :].bitcast(I32).rearrange("r (j n) -> r j n", j=G),
+                in_=wt_scales[:, 4 * quad : 4 * quad + 4, :].bitcast(I32).rearrange("j r n -> r j n"),
+            )
         load_w(0)
         load_e(1)
-        load_v(1, 0, 512)
-        load_v(0, 512, 1024)
-        load_v(1, 512, 1024)
+        load_v(1, 0)
+        load_v(0, 1)
+        load_e(2)
+        load_v(1, 1)
         for g in range(2):
             nc.sync.dma_start(
                 out=c_sb[:, g, :, :],
                 in_=c[512 * g : 512 * g + 512, :].rearrange("(p t) r -> p t r", t=4),
             )
         for j in range(1, G):
-            load_e(2 * j)
+            if j > 1:
+                load_e(2 * j)
             load_w(j)
             load_e(2 * j + 1)
-            load_v(2 * j, 0, F)
-            load_v(2 * j + 1, 0, F)
+            load_v(2 * j)
+            load_v(2 * j + 1)
 
         e_grp = {}
 
-        def e_transpose(n, half):
+        def e_transpose(n, half, head=False):
             if half == 0:
                 eg = work.tile([P, 2048], BF16, align_bytes=64, name="eg")
                 e_grp[n] = eg
-            et = psum.tile([P, 2, 2, P], F32, bufs=1, name="et")
+            if head:
+                et = psum.tile([P, 2, 2, P], F32, name="ob")
+            else:
+                et = psum.tile([P, 2, 2, P], F32, bufs=1, name="et")
             words = e_sb[n][:].bitcast(F32)
             for tt in range(2):
                 for u in range(2):
@@ -140,16 +153,21 @@ def tile_pact_threshold_grad_s14_kernel(tc, e, wt_words, wt_scales, v, beta, c, 
             nc.vector.tensor_copy(out=bcol_f[:], in_=yt[:, 0, 0:32])
 
         def beta_rows(j):
+            if j in (1, 2):
+                bt = psum.tile([P, 8, P], BF16, name="da")
+            else:
+                bt = psum.tile([P, 8, P], BF16, bufs=1, name="et")
             for q in range(2):
                 count = max(len(a_blocks(4 * j + 2 * q)), len(a_blocks(4 * j + 2 * q + 1)))
+                for b in range(count):
+                    i = 4 * q + b
+                    nc.tensor.transpose(
+                        bt[:, i, :], bcol_b[:, 8 * j + i : 8 * j + i + 1].to_broadcast([P, P]), ident_b[:]
+                    )
                 if count:
-                    yt = psum.tile([P, 4, P], BF16, name="yt")
-                    for b in range(count):
-                        i = 8 * j + 4 * q + b
-                        nc.tensor.transpose(yt[:, b, :], bcol_b[:, i : i + 1].to_broadcast([P, P]), ident_b[:])
                     nc.scalar.copy(
                         out=betab[j][:, 512 * q : 512 * q + P * count],
-                        in_=yt[:, 0:count, :].rearrange("p b f -> p (b f)"),
+                        in_=bt[:, 4 * q : 4 * q + count, :].rearrange("p b f -> p (b f)"),
                     )
 
         mks, mbs, zs, ys, yts = {}, {}, {}, {}, {}
@@ -158,9 +176,9 @@ def tile_pact_threshold_grad_s14_kernel(tc, e, wt_words, wt_scales, v, beta, c, 
             width = P * len(a_blocks(k))
             if width:
                 j, q, g = slot_of(k)
-                mk = work.tile([P, 4, 512], BF16, align_bytes=64, bufs=1, name="mk")
+                mk = work.tile([P, 4, 512], BF16, align_bytes=64, name="mk")
                 nc.vector.tensor_scalar(
-                    out=mk[:, :, 0:width], in0=v_sb[2 * j + g][:, :, 512 * q : 512 * q + width],
+                    out=mk[:, :, 0:width], in0=v_sb[2 * j + g, q][:, :, 0:width],
                     scalar1=0.0, scalar2=None, op0=ALU.is_ge,
                 )
                 mks[k] = mk
@@ -169,8 +187,9 @@ def tile_pact_threshold_grad_s14_kernel(tc, e, wt_words, wt_scales, v, beta, c, 
             width = P * len(a_blocks(k))
             if width:
                 j, q, g = slot_of(k)
-                mb = work.tile([P, 4, 512], BF16, align_bytes=64, name="mb")
-                nc.vector.tensor_tensor(
+                mb = work.tile([P, 4, 512], BF16, align_bytes=64, bufs=3, name="mb")
+                eng = nc.vector if k in (0, 1, 15) else nc.gpsimd
+                eng.tensor_tensor(
                     out=mb[:, :, 0:width], in0=mks[k][:, :, 0:width],
                     in1=betab[j][:, 512 * q : 512 * q + width].unsqueeze(1).to_broadcast([P, 4, width]),
                     op=ALU.mult,
@@ -215,7 +234,7 @@ def tile_pact_threshold_grad_s14_kernel(tc, e, wt_words, wt_scales, v, beta, c, 
                 rhs=e_codes[n][:].bitcast(FP8), rhs_scale=e_scales[n][:],
                 start=True, stop=True,
             )
-            y = work.tile([P, 512], BF16, align_bytes=64, bufs=6, name="y")
+            y = work.tile([P, 512], BF16, align_bytes=64, bufs=4, name="y")
             i = 8 * j + fb
             nc.scalar.activation(out=y[:], in_=db[:], func=ACT.Copy, scale=bcol_f[:, i : i + 1])
             ys[k, b] = y
@@ -228,10 +247,9 @@ def tile_pact_threshold_grad_s14_kernel(tc, e, wt_words, wt_scales, v, beta, c, 
 
         def gate_b(k, b):
             j, q, g = slot_of(k)
-            lo = 512 * q + P * b
             nc.vector.scalar_tensor_tensor(
                 out=zs[k][:, P * b : P * b + P, :],
-                in0=v_sb[2 * j + g][:, :, lo : lo + P].rearrange("p t f -> p f t"),
+                in0=v_sb[2 * j + g, q][:, :, P * b : P * b + P].rearrange("p t f -> p f t"),
                 scalar=0.0,
                 in1=yts[k, b][:].rearrange("p t f -> p f t"),
                 op0=ALU.is_ge, op1=ALU.mult,
@@ -253,13 +271,19 @@ def tile_pact_threshold_grad_s14_kernel(tc, e, wt_words, wt_scales, v, beta, c, 
         c_scales = keep.tile([P, 2 * R], U8, align_bytes=64, name="c_scales")
         c_grp = keep.tile([P, 2, R, 4], BF16, align_bytes=64, name="c_grp")
 
-        def c_copy(g, half):
-            cols = slice(256 * half, 256 * half + 256)
-            nc.scalar.copy(out=c_grp[:, g, cols, :], in_=c_sb[:, g, :, cols].rearrange("p t r -> p r t"))
+        def c_copy(g, part, on_vector):
+            cols = slice(128 * part, 128 * part + 128)
+            dst, src = c_grp[:, g, cols, :], c_sb[:, g, :, cols].rearrange("p t r -> p r t")
+            if on_vector:
+                nc.vector.tensor_copy(out=dst, in_=src)
+            else:
+                nc.scalar.copy(out=dst, in_=src)
 
-        def c_quant():
+        def c_quant(g):
+            cols = slice(R * g, R * g + R)
             nc.vector.quantize_mx(
-                out=c_codes[:].bitcast(FP8), scales=c_scales[:], in_=c_grp[:].rearrange("p g r t -> p (g r t)")
+                out=c_codes[:, cols].bitcast(FP8), scales=c_scales[:, cols],
+                in_=c_grp[:, g, :, :].rearrange("p r t -> p (r t)"),
             )
 
         def second(pair, rt, on_vector, lo=0, hi=512):
@@ -274,7 +298,7 @@ def tile_pact_threshold_grad_s14_kernel(tc, e, wt_words, wt_scales, v, beta, c, 
                     rhs=z_codes[k][:, lo:hi].bitcast(FP8), rhs_scale=z_scales[k][:, lo:hi],
                     start=(g == 0), stop=(g == 1),
                 )
-            ot = work.tile([P, 512], F32, bufs=6, name="ot")
+            ot = work.tile([P, 512], F32, bufs=10, name="ot")
             if on_vector:
                 nc.vector.tensor_copy(out=ot[:, lo:hi], in_=ob[:, lo:hi])
             else:
@@ -283,22 +307,23 @@ def tile_pact_threshold_grad_s14_kernel(tc, e, wt_words, wt_scales, v, beta, c, 
                 out=out[j, P * rt : P * rt + P, 512 * q + lo : 512 * q + hi], in_=ot[:, lo:hi]
             )
 
-        def e_head(n, on_vector):
+        def e_head(n):
             for half in range(2):
-                et = e_transpose(n, half)
-                e_copy(n, half, et, on_vector and half == 1)
+                et = e_transpose(n, half, True)
+                e_copy(n, half, et, half == 1)
 
-        e_head(0, True)
+        e_head(0)
         beta_columns()
-        beta_rows(0)
         mask(0)
         e_quant(0)
+        for j in range(G):
+            beta_rows(j)
         mask_beta(0)
 
         for k in range(N_SLOT):
             job = None
-            if k < 12:
-                job = (2 * (k // 4 + 1) + (k % 4) // 2, k % 2)
+            if 1 <= k < 13:
+                job = (2 * ((k - 1) // 4 + 1) + ((k - 1) % 4) // 2, (k - 1) % 2)
                 et = e_transpose(job[0], job[1])
             late = b_blocks(k - 1)
             for b in late[:2]:
@@ -306,8 +331,6 @@ def tile_pact_threshold_grad_s14_kernel(tc, e, wt_words, wt_scales, v, beta, c, 
             if job:
                 e_copy(job[0], job[1], et)
             open_z(k)
-            if k:
-                mask(k + 1)
             groups = []
             if 3 <= k < 15:
                 groups = [((k - 3) // 2, 2 * ((k - 3) % 2) + i) for i in range(2)]
@@ -315,6 +338,9 @@ def tile_pact_threshold_grad_s14_kernel(tc, e, wt_words, wt_scales, v, beta, c, 
                 groups = [(6, rt) for rt in range(4)]
             now_a, now_b = a_blocks(k), b_blocks(k)
             for r in range(4):
+                if k == 3 and r == 2:
+                    c_quant(0)
+                    c_quant(1)
                 if r < len(now_b):
                     mm_b(k, now_b[r])
                 if r < len(now_a):
@@ -325,28 +351,35 @@ def tile_pact_threshold_grad_s14_kernel(tc, e, wt_words, wt_scales, v, beta, c, 
                         y_transpose(k - 1, late[r + 2])
                 if r < len(now_a):
                     gate_a(k, now_a[r], da)
+                if r == 1 and job and job[1] == 1:
+                    e_quant(job[0])
                 if k == 15 and r == 2:
                     z_quant(14)
                 if k == 15 and r == 3:
                     z_quant(15, 0, 256)
-                if r < len(groups):
+                if r < len(groups) and k > 3:
                     second(groups[r][0], groups[r][1], False)
+            if k == 3:
+                for pair, rt in groups:
+                    second(pair, rt, False)
             if k == 0:
-                e_head(1, False)
+                e_head(1)
                 mask(1)
                 e_quant(1)
+                mask_beta(1)
             if 1 <= k < 15:
                 z_quant(k - 1)
-            if job and job[1] == 1:
-                e_quant(job[0])
-            if k in (1, 2):
-                c_copy(k - 1, 0)
-                c_copy(k - 1, 1)
+            mask(k + 2)
+            mask_beta(k + 2)
+            if k == 1:
+                for part in range(3):
+                    c_copy(0, part, False)
             if k == 2:
-                c_quant()
-            if k in (1, 5, 9):
-                beta_rows(k // 4 + 1)
-            mask_beta(k + 1)
+                c_copy(0, 3, False)
+                c_copy(1, 0, False)
+                c_copy(1, 1, False)
+                c_copy(1, 2, True)
+                c_copy(1, 3, True)
         z_quant(15, 256, 512)
         for half in range(2):
             for rt in range(4):

@@ -18,7 +18,14 @@ ACT = mybir.ActivationFunctionType
 
 P = 128
 N_SLOT = 16
-NB = [2] * 15 + [0]
+NB = [2] * 15 + [4]
+QUANT = {14: [11, 12], 15: [13]}
+TAIL_QUANT = [14]
+TAIL_SPLIT = True
+E_JOBS = {1: [(2, 0)], 2: [(2, 1), (3, 0)], 3: [(3, 1), (4, 0)], 4: [(4, 1)], 5: [(5, 0)], 6: [(5, 1)], 7: [(6, 0)], 8: [(6, 1)], 9: [(7, 0)], 10: [(7, 1)]}
+E_QUANT = {3: 2, 4: 3, 6: 4, 8: 5, 10: 6, 12: 7}
+C_PARTS = {1: [(0, 0, 1), (0, 1, 0)], 2: [(0, 2, 1), (0, 3, 1), (1, 0, 1)], 3: [(1, 1, 0), (1, 2, 1), (1, 3, 0)]}
+SECOND = [0] * 4 + [2] * 10 + [3, 3]
 
 
 def tile_pact_threshold_grad_s14_kernel(tc, e, wt_words, wt_scales, v, beta, c, out):
@@ -32,12 +39,22 @@ def tile_pact_threshold_grad_s14_kernel(tc, e, wt_words, wt_scales, v, beta, c, 
         def slot_of(k):
             return k // 4, (k % 4) // 2, k % 2
 
+        planes = {}
+        planes[0] = keep.tile([P, F], U8, align_bytes=64, name="planes0")
+        plane_rest = keep.tile([P, 3 * F], U8, align_bytes=64, name="plane_rest")
+        for j in range(1, G):
+            planes[j] = plane_rest[:, F * (j - 1) : F * j]
+        nc.vector.memset(planes[0][:].bitcast(I32), 0)
         brow = keep.tile([P, P], BF16, align_bytes=64, name="brow")
         nc.vector.memset(brow[:], 0.0)
-        planes = keep.tile([P, G * F], U8, align_bytes=64, name="planes")
-        nc.vector.memset(planes[:].bitcast(I32), 0)
         warm = keep.tile([P, 2], F32, name="warm")
         nc.vector.memset(warm[:], 0.0)
+        nc.vector.memset(plane_rest[:].bitcast(I32), 0)
+        w_sb = {}
+        for j in range(G):
+            w_sb[j] = keep.tile([P, 2 * F], U8, align_bytes=64, name="w_sb%d" % j)
+        nc.gpsimd.dma_start(out=w_sb[0][:].bitcast(I32), in_=wt_words[0].bitcast(I32))
+        nc.gpsimd.dma_start(out=brow[0:32, :], in_=beta.rearrange("j (b f) -> (j b) f", f=P))
         ident_f = keep.tile([P, P], F32, align_bytes=64, name="ident_f")
         make_identity(nc, ident_f[:])
         ident_b = keep.tile([P, P], BF16, align_bytes=64, name="ident_b")
@@ -45,7 +62,7 @@ def tile_pact_threshold_grad_s14_kernel(tc, e, wt_words, wt_scales, v, beta, c, 
 
         nc.scalar.activation(out=warm[:, 1:2], in_=warm[:, 0:1], func=ACT.Copy, scale=1.0)
 
-        e_sb, v_sb, w_sb, e_codes, e_scales, betab = {}, {}, {}, {}, {}, {}
+        e_sb, v_sb, e_codes, e_scales, betab = {}, {}, {}, {}, {}
         for n in range(8):
             e_sb[n] = keep.tile([P, 4 * O], BF16, align_bytes=64, name="e_sb%d" % n)
             if n < 2:
@@ -59,15 +76,15 @@ def tile_pact_threshold_grad_s14_kernel(tc, e, wt_words, wt_scales, v, beta, c, 
             e_codes[n] = keep.tile([P, 512], U32, align_bytes=64, name="e_codes%d" % n)
             e_scales[n] = keep.tile([P, 512], U8, align_bytes=64, name="e_scales%d" % n)
         for j in range(G):
-            w_sb[j] = keep.tile([P, 2 * F], U8, align_bytes=64, name="w_sb%d" % j)
             betab[j] = keep.tile([P, F], BF16, align_bytes=64, name="betab%d" % j)
         c_sb = keep.tile([P, 2, 4, R], BF16, align_bytes=64, name="c_sb")
 
-        def load_e(n):
+        def load_e(n, half=None):
             j, g = n // 2, n % 2
+            rows = slice(0, 4) if half is None else slice(2 * half, 2 * half + 2)
             nc.sync.dma_start(
-                out=e_sb[n][:].rearrange("p (t k) -> p t k", t=4),
-                in_=e[j, 512 * g : 512 * g + 512, :].rearrange("(p t) k -> p t k", t=4),
+                out=e_sb[n][:].rearrange("p (t k) -> p t k", t=4)[:, rows, :],
+                in_=e[j, 512 * g : 512 * g + 512, :].rearrange("(p t) k -> p t k", t=4)[:, rows, :],
             )
 
         def load_v(n, q=None):
@@ -81,41 +98,59 @@ def tile_pact_threshold_grad_s14_kernel(tc, e, wt_words, wt_scales, v, beta, c, 
         def load_w(j):
             nc.sync.dma_start(out=w_sb[j][:].bitcast(I32), in_=wt_words[j].bitcast(I32))
 
-        load_e(0)
-        nc.sync.dma_start(out=brow[0:32, :], in_=beta.rearrange("j (b f) -> (j b) f", f=P))
-        load_v(0, 0)
-        for quad in range(4):
-            nc.sync.dma_start(
-                out=planes[32 * quad : 32 * quad + 4, :].bitcast(I32).rearrange("r (j n) -> r j n", j=G),
-                in_=wt_scales[:, 4 * quad : 4 * quad + 4, :].bitcast(I32).rearrange("j r n -> r j n"),
-            )
-        load_w(0)
-        load_e(1)
-        load_v(1, 0)
-        load_v(0, 1)
-        load_e(2)
-        load_v(1, 1)
-        for g in range(2):
+        def load_c(g):
             nc.sync.dma_start(
                 out=c_sb[:, g, :, :],
                 in_=c[512 * g : 512 * g + 512, :].rearrange("(p t) r -> p t r", t=4),
             )
+
+        def load_planes_first():
+            for quad in range(4):
+                nc.sync.dma_start(
+                    out=planes[0][32 * quad : 32 * quad + 4, :].bitcast(I32),
+                    in_=wt_scales[0, 4 * quad : 4 * quad + 4, :].bitcast(I32),
+                )
+
+        def load_planes_rest():
+            for quad in range(4):
+                nc.sync.dma_start(
+                    out=plane_rest[32 * quad : 32 * quad + 4, :].bitcast(I32).rearrange("r (j n) -> r j n", j=3),
+                    in_=wt_scales[1:4, 4 * quad : 4 * quad + 4, :].bitcast(I32).rearrange("j r n -> r j n"),
+                )
+
+        load_e(0, 0)
+        load_e(0, 1)
+        load_planes_first()
+        load_e(1)
+        load_v(0, 0)
+        load_v(1, 0)
+        load_e(2)
+        load_v(0, 1)
+        load_c(0)
+        load_e(3)
+        load_v(1, 1)
+        load_c(1)
+        load_e(4)
         for j in range(1, G):
-            if j > 1:
-                load_e(2 * j)
             load_w(j)
-            load_e(2 * j + 1)
+            if j == 1:
+                load_planes_rest()
             load_v(2 * j)
+            for n in (2 * j + 3, 2 * j + 4):
+                if n < 2 * G:
+                    load_e(n)
             load_v(2 * j + 1)
 
         e_grp = {}
 
-        def e_transpose(n, half, head=False):
+        def e_transpose(n, half, tag=None):
             if half == 0:
                 eg = work.tile([P, 2048], BF16, align_bytes=64, name="eg")
                 e_grp[n] = eg
-            if head:
+            if tag == "ob":
                 et = psum.tile([P, 2, 2, P], F32, name="ob")
+            elif tag == "da":
+                et = psum.tile([P, 2, 2, P], F32, name="da")
             else:
                 et = psum.tile([P, 2, 2, P], F32, bufs=1, name="et")
             words = e_sb[n][:].bitcast(F32)
@@ -147,58 +182,31 @@ def tile_pact_threshold_grad_s14_kernel(tc, e, wt_words, wt_scales, v, beta, c, 
         bcol_f = keep.tile([P, 32], F32, name="bcol_f")
 
         def beta_columns():
-            yt = psum.tile([P, 4, P], BF16, name="yt")
-            nc.tensor.transpose(yt[:, 0, :], brow[:], ident_b[:])
+            yt = psum.tile([P, 4, 2 * P], BF16, bufs=1, name="yt")
+            nc.tensor.transpose(yt[:, 0, 0:P], brow[:], ident_b[:])
             nc.scalar.copy(out=bcol_b[:], in_=yt[:, 0, 0:32])
             nc.vector.tensor_copy(out=bcol_f[:], in_=yt[:, 0, 0:32])
 
         def beta_rows(j):
-            if j in (1, 2):
-                bt = psum.tile([P, 8, P], BF16, name="da")
-            else:
-                bt = psum.tile([P, 8, P], BF16, bufs=1, name="et")
+            bt = psum.tile([P, 2, 4, P], BF16, name="ob")
+            count = max(len(a_blocks(k)) for k in range(4 * j, 4 * j + 4))
             for q in range(2):
-                count = max(len(a_blocks(4 * j + 2 * q)), len(a_blocks(4 * j + 2 * q + 1)))
                 for b in range(count):
-                    i = 4 * q + b
-                    nc.tensor.transpose(
-                        bt[:, i, :], bcol_b[:, 8 * j + i : 8 * j + i + 1].to_broadcast([P, P]), ident_b[:]
-                    )
-                if count:
-                    nc.scalar.copy(
-                        out=betab[j][:, 512 * q : 512 * q + P * count],
-                        in_=bt[:, 4 * q : 4 * q + count, :].rearrange("p b f -> p (b f)"),
-                    )
+                    i = 8 * j + 4 * q + b
+                    nc.tensor.transpose(bt[:, q, b, :], bcol_b[:, i : i + 1].to_broadcast([P, P]), ident_b[:])
+            nc.scalar.copy(
+                out=betab[j][:].rearrange("p (q b f) -> p q b f", q=2, b=4)[:, :, 0:count, :],
+                in_=bt[:, :, 0:count, :],
+            )
 
-        mks, mbs, zs, ys, yts = {}, {}, {}, {}, {}
-
-        def mask(k):
-            width = P * len(a_blocks(k))
-            if width:
-                j, q, g = slot_of(k)
-                mk = work.tile([P, 4, 512], BF16, align_bytes=64, name="mk")
-                nc.vector.tensor_scalar(
-                    out=mk[:, :, 0:width], in0=v_sb[2 * j + g, q][:, :, 0:width],
-                    scalar1=0.0, scalar2=None, op0=ALU.is_ge,
-                )
-                mks[k] = mk
-
-        def mask_beta(k):
-            width = P * len(a_blocks(k))
-            if width:
-                j, q, g = slot_of(k)
-                mb = work.tile([P, 4, 512], BF16, align_bytes=64, bufs=3, name="mb")
-                eng = nc.vector if k in (0, 1, 15) else nc.gpsimd
-                eng.tensor_tensor(
-                    out=mb[:, :, 0:width], in0=mks[k][:, :, 0:width],
-                    in1=betab[j][:, 512 * q : 512 * q + width].unsqueeze(1).to_broadcast([P, 4, width]),
-                    op=ALU.mult,
-                )
-                mbs[k] = mb
+        mds, zs, ys, yts = {}, {}, {}, {}
 
         def open_z(k):
-            z = work.tile([P, 512, 4], BF16, align_bytes=64, bufs=3, name="z")
+            z = work.tile([P, 512, 4], BF16, align_bytes=64, bufs=5, name="z")
             zs[k] = z
+            if a_blocks(k):
+                md = work.tile([P, 256, 4], F32, align_bytes=64, bufs=3, name="md")
+                mds[k] = md
 
         def mm_a(k, b):
             j, q, g = slot_of(k)
@@ -210,27 +218,46 @@ def tile_pact_threshold_grad_s14_kernel(tc, e, wt_words, wt_scales, v, beta, c, 
                     out=da[:, t, :],
                     lhsT=e_codes[n][:, cols].bitcast(FP8), lhsT_scale=e_scales[n][:, cols],
                     rhs=w_sb[j][:, 256 * fb : 256 * fb + 256].bitcast(FP4),
-                    rhs_scale=planes[:, F * j + P * fb : F * j + P * fb + P],
+                    rhs_scale=planes[j][:, P * fb : P * fb + P],
                     start=True, stop=True,
                 )
             return da
 
         def gate_a(k, b, da):
-            nc.vector.tensor_tensor(
-                out=zs[k][:, P * b : P * b + P, :],
-                in0=da[:].rearrange("p t f -> p f t"),
-                in1=mbs[k][:, :, P * b : P * b + P].rearrange("p t f -> p f t"),
-                op=ALU.mult,
+            j, q, g = slot_of(k)
+            nc.vector.scalar_tensor_tensor(
+                out=mds[k][:, P * b : P * b + P, :],
+                in0=v_sb[2 * j + g, q][:, :, P * b : P * b + P].rearrange("p t f -> p f t"),
+                scalar=0.0,
+                in1=da[:].rearrange("p t f -> p f t"),
+                op0=ALU.is_ge, op1=ALU.mult,
             )
+
+        def scale_a(k):
+            j, q, g = slot_of(k)
+            n = P * len(a_blocks(k))
+            if n:
+                nc.gpsimd.tensor_tensor(
+                    out=zs[k][:, 0:n, :], in0=mds[k][:, 0:n, :],
+                    in1=betab[j][:, 512 * q : 512 * q + n].unsqueeze(2).to_broadcast([P, n, 4]),
+                    op=ALU.mult,
+                )
+
+        def hold_gpsimd(k):
+            tick = work.tile([P, 1], U32, name="tick")
+            nc.gpsimd.tensor_copy(out=tick[:], in_=z_codes[k][:, 511:512])
 
         def mm_b(k, b):
             j, q, g = slot_of(k)
             n, fb = 2 * j + g, 4 * q + b
-            db = psum.tile([P, 512], F32, bufs=1, name="db")
+            if b_blocks(k).index(b) < 2:
+                db = psum.tile([P, 512], F32, name="db")
+            else:
+                db = psum.tile([P, 512], F32, name="da")
             nc.tensor.matmul_mx(
                 out=db[:],
                 lhsT=w_sb[j][:, 256 * fb : 256 * fb + 256].bitcast(FP4),
-                lhsT_scale=planes[:, F * j + P * fb : F * j + P * fb + P],
+                lhsT_scale=planes[j][:, P * fb : P * fb + P],
                 rhs=e_codes[n][:].bitcast(FP8), rhs_scale=e_scales[n][:],
                 start=True, stop=True,
             )
@@ -239,19 +266,31 @@ def tile_pact_threshold_grad_s14_kernel(tc, e, wt_words, wt_scales, v, beta, c, 
             nc.scalar.activation(out=y[:], in_=db[:], func=ACT.Copy, scale=bcol_f[:, i : i + 1])
             ys[k, b] = y
 
-        def y_transpose(k, b):
-            yt = psum.tile([P, 4, P], BF16, name="yt")
-            for t in range(4):
-                nc.tensor.transpose(yt[:, t, :], ys[k, b][:, P * t : P * t + P], ident_b[:])
-            yts[k, b] = yt
+        def y_groups(k):
+            blocks = b_blocks(k)
+            return [blocks[i : i + 2] for i in range(0, len(blocks), 2)]
 
-        def gate_b(k, b):
+        def y_transpose(k, group, bank="yt"):
+            if bank == "yt":
+                yt = psum.tile([P, 4, 2 * P], BF16, bufs=1, name="yt")
+            else:
+                yt = psum.tile([P, 4, 2 * P], BF16, bufs=1, name="et")
+            for i, b in enumerate(group):
+                for t in range(4):
+                    nc.tensor.transpose(
+                        yt[:, t, P * i : P * i + P], ys[k, b][:, P * t : P * t + P], ident_b[:]
+                    )
+            yts[k, group[0]] = yt
+
+        def gate_b(k, group):
             j, q, g = slot_of(k)
+            n = P * len(group)
+            cols = slice(P * group[0], P * group[0] + n)
             nc.vector.scalar_tensor_tensor(
-                out=zs[k][:, P * b : P * b + P, :],
-                in0=v_sb[2 * j + g, q][:, :, P * b : P * b + P].rearrange("p t f -> p f t"),
+                out=zs[k][:, cols, :],
+                in0=v_sb[2 * j + g, q][:, :, cols].rearrange("p t f -> p f t"),
                 scalar=0.0,
-                in1=yts[k, b][:].rearrange("p t f -> p f t"),
+                in1=yts[k, group[0]][:, :, 0:n].rearrange("p t f -> p f t"),
                 op0=ALU.is_ge, op1=ALU.mult,
             )
 
@@ -286,9 +325,13 @@ def tile_pact_threshold_grad_s14_kernel(tc, e, wt_words, wt_scales, v, beta, c, 
                 in_=c_grp[:, g, :, :].rearrange("p r t -> p (r t)"),
             )
 
-        def second(pair, rt, on_vector, lo=0, hi=512):
-            j, q = pair // 2, pair % 2
-            ob = psum.tile([P, 512], F32, name="ob")
+        def second(pair, rt, lo=0, hi=512, bank="ob"):
+            if bank == "ob":
+                ob = psum.tile([P, 512], F32, name="ob")
+            elif bank == "da":
+                ob = psum.tile([P, 512], F32, name="da")
+            else:
+                ob = psum.tile([P, 512], F32, name="db")
             for g in range(2):
                 k = 2 * pair + g
                 cols = slice(R * g + P * rt, R * g + P * rt + P)
@@ -298,6 +341,10 @@ def tile_pact_threshold_grad_s14_kernel(tc, e, wt_words, wt_scales, v, beta, c, 
                     rhs=z_codes[k][:, lo:hi].bitcast(FP8), rhs_scale=z_scales[k][:, lo:hi],
                     start=(g == 0), stop=(g == 1),
                 )
+            return ob
+
+        def finish(pair, rt, ob, on_vector, lo=0, hi=512):
+            j, q = pair // 2, pair % 2
             ot = work.tile([P, 512], F32, bufs=10, name="ot")
             if on_vector:
                 nc.vector.tensor_copy(out=ot[:, lo:hi], in_=ob[:, lo:hi])
@@ -307,80 +354,74 @@ def tile_pact_threshold_grad_s14_kernel(tc, e, wt_words, wt_scales, v, beta, c, 
                 out=out[j, P * rt : P * rt + P, 512 * q + lo : 512 * q + hi], in_=ot[:, lo:hi]
             )
 
-        def e_head(n):
-            for half in range(2):
-                et = e_transpose(n, half, True)
-                e_copy(n, half, et, half == 1)
-
-        e_head(0)
+        for half in range(2):
+            et = e_transpose(0, half, "ob")
+            e_copy(0, half, et, half == 1)
         beta_columns()
-        mask(0)
         e_quant(0)
-        for j in range(G):
-            beta_rows(j)
-        mask_beta(0)
+        for half in range(2):
+            et = e_transpose(1, half, "da")
+            e_copy(1, half, et, half == 1)
+        e_quant(1)
 
         for k in range(N_SLOT):
-            job = None
-            if 1 <= k < 13:
-                job = (2 * ((k - 1) // 4 + 1) + ((k - 1) % 4) // 2, (k - 1) % 2)
-                et = e_transpose(job[0], job[1])
-            late = b_blocks(k - 1)
-            for b in late[:2]:
-                y_transpose(k - 1, b)
-            if job:
-                e_copy(job[0], job[1], et)
+            late, now_a, now_b = y_groups(k - 1), a_blocks(k), b_blocks(k)
+            first = sum(SECOND[:k])
+            groups = [(i // 4, i % 4) for i in range(first, first + SECOND[k])]
             open_z(k)
-            groups = []
-            if 3 <= k < 15:
-                groups = [((k - 3) // 2, 2 * ((k - 3) % 2) + i) for i in range(2)]
-            if k == 15:
-                groups = [(6, rt) for rt in range(4)]
-            now_a, now_b = a_blocks(k), b_blocks(k)
-            for r in range(4):
-                if k == 3 and r == 2:
-                    c_quant(0)
-                    c_quant(1)
-                if r < len(now_b):
-                    mm_b(k, now_b[r])
-                if r < len(now_a):
-                    da = mm_a(k, now_a[r])
-                if r < len(late):
-                    gate_b(k - 1, late[r])
-                    if r + 2 < len(late):
-                        y_transpose(k - 1, late[r + 2])
-                if r < len(now_a):
-                    gate_a(k, now_a[r], da)
-                if r == 1 and job and job[1] == 1:
-                    e_quant(job[0])
-                if k == 15 and r == 2:
-                    z_quant(14)
-                if k == 15 and r == 3:
-                    z_quant(15, 0, 256)
-                if r < len(groups) and k > 3:
-                    second(groups[r][0], groups[r][1], False)
-            if k == 3:
-                for pair, rt in groups:
-                    second(pair, rt, False)
-            if k == 0:
-                e_head(1)
-                mask(1)
-                e_quant(1)
-                mask_beta(1)
-            if 1 <= k < 15:
-                z_quant(k - 1)
-            mask(k + 2)
-            mask_beta(k + 2)
-            if k == 1:
-                for part in range(3):
-                    c_copy(0, part, False)
-            if k == 2:
-                c_copy(0, 3, False)
-                c_copy(1, 0, False)
-                c_copy(1, 1, False)
-                c_copy(1, 2, True)
-                c_copy(1, 3, True)
+            for group, bank in zip(late, ("yt", "et")):
+                y_transpose(k - 1, group, bank)
+            for i, (n, half) in enumerate(E_JOBS.get(k, [])):
+                e_copy(n, half, e_transpose(n, half, "ob" if i else None))
+            if k in (1, 2):
+                beta_rows(k)
+            if k in E_QUANT:
+                e_quant(E_QUANT[k])
+            if k in (3, 4):
+                c_quant(k - 3)
+            for i in QUANT.get(k, [k - 3] if k >= 3 else []):
+                z_quant(i)
+                hold_gpsimd(i)
+            if k >= 1:
+                scale_a(k - 1)
+            for group in late:
+                gate_b(k - 1, group)
+            for b in now_b[:2]:
+                mm_b(k, b)
+            obs = []
+            rest = now_a + now_b[2:]
+            for i in range(max(len(rest), len(groups))):
+                if i < len(now_a):
+                    da = mm_a(k, now_a[i])
+                    gate_a(k, now_a[i], da)
+                elif i < len(rest):
+                    mm_b(k, rest[i])
+                if i < len(groups):
+                    obs.append(second(*groups[i]))
+            for i in range(len(groups)):
+                finish(*groups[i], obs[i], False)
+            if k in (0, 2):
+                beta_rows(k + k // 2)
+            for g, part, on_vector in C_PARTS.get(k, []):
+                c_copy(g, part, on_vector)
+        for i in TAIL_QUANT:
+            z_quant(i)
+        tail = [(i // 4, i % 4) for i in range(sum(SECOND), 28)]
+        for i, group in enumerate(y_groups(15)):
+            y_transpose(15, group, ("yt", "et")[i])
+            if TAIL_SPLIT and i == 0:
+                for unit in tail:
+                    finish(*unit, second(*unit), False)
+        if not TAIL_SPLIT:
+            for unit in tail:
+                finish(*unit, second(*unit), False)
+        for i, group in enumerate(y_groups(15)):
+            gate_b(15, group)
+            if i < len(y_groups(15)) - 1 or len(y_groups(15)) == 1:
+                z_quant(15, 0, 256)
         z_quant(15, 256, 512)
         for half in range(2):
             for rt in range(4):
-                second(7, rt, rt % 2 == 1, 256 * half, 256 * half + 256)
+                cols = (256 * half, 256 * half + 256)
+                bank = ("ob", "da", "ob", "db")[rt]
+                finish(7, rt, second(7, rt, *cols, bank), rt % 2 == 1, *cols)

@@ -19,12 +19,20 @@ ACT = mybir.ActivationFunctionType
 P = 128
 N_SLOT = 16
 NB = [2] * 15 + [4]
-QUANT = {14: [11, 12], 15: [13]}
+QUANT = {2: [0], 3: [1], 4: [], 14: [11, 12], 15: [13]}
 TAIL_QUANT = [14]
-TAIL_SPLIT = True
-E_JOBS = {1: [(2, 0)], 2: [(2, 1), (3, 0)], 3: [(3, 1), (4, 0)], 4: [(4, 1)], 5: [(5, 0)], 6: [(5, 1)], 7: [(6, 0)], 8: [(6, 1)], 9: [(7, 0)], 10: [(7, 1)]}
-E_QUANT = {3: 2, 4: 3, 6: 4, 8: 5, 10: 6, 12: 7}
-C_PARTS = {1: [(0, 0, 1), (0, 1, 0)], 2: [(0, 2, 1), (0, 3, 1), (1, 0, 1)], 3: [(1, 1, 0), (1, 2, 1), (1, 3, 0)]}
+V15 = [0, 1]
+TAIL_PE = "TssTGG"
+TAIL_BANK = ["da", "db"]
+TAIL_V = []
+GDONE = []
+ORDER = "BABAss"
+EARLY = False
+HEAD_V = [0, 1]
+C_QUANT = [4, 4]
+E_JOBS = {1: [(2, 0), (2, 1)], 2: [(3, 0)], 3: [(3, 1)], 4: [(4, 0), (4, 1)], 6: [(5, 0), (5, 1)], 8: [(6, 0), (6, 1)], 10: [(7, 0), (7, 1)]}
+E_QUANT = {2: 2, 4: 3, 6: 4, 8: 5, 10: 6, 12: 7}
+C_PARTS = {1: [(0, 3, 0), (0, 0, 0)], 2: [(1, 3, 1), (0, 1, 0)], 3: [(1, 2, 1), (0, 2, 0), (1, 1, 0), (1, 0, 0)]}
 SECOND = [0] * 4 + [2] * 10 + [3, 3]
 
 
@@ -202,32 +210,35 @@ def tile_pact_threshold_grad_s14_kernel(tc, e, wt_words, wt_scales, v, beta, c, 
         mds, zs, ys, yts = {}, {}, {}, {}
 
         def open_z(k):
-            z = work.tile([P, 512, 4], BF16, align_bytes=64, bufs=5, name="z")
+            z = work.tile([P, 512, 4], BF16, align_bytes=64, name="z")
             zs[k] = z
+
+        def open_md(k):
             if a_blocks(k):
-                md = work.tile([P, 256, 4], F32, align_bytes=64, bufs=3, name="md")
+                md = work.tile([P, 2, 256, 2], F32, align_bytes=64, bufs=3, name="md")
                 mds[k] = md
 
-        def mm_a(k, b):
+        def mm_a(k, h):
             j, q, g = slot_of(k)
-            n, fb = 2 * j + g, 4 * q + b
-            da = psum.tile([P, 4, P], F32, name="da")
-            for t in range(4):
+            n, f0 = 2 * j + g, 512 * q
+            da = psum.tile([P, 2, 2 * P], F32, name="da")
+            for r in range(2):
+                t = 2 * h + r
                 cols = slice(P * t, P * t + P)
                 nc.tensor.matmul_mx(
-                    out=da[:, t, :],
+                    out=da[:, r, :],
                     lhsT=e_codes[n][:, cols].bitcast(FP8), lhsT_scale=e_scales[n][:, cols],
-                    rhs=w_sb[j][:, 256 * fb : 256 * fb + 256].bitcast(FP4),
-                    rhs_scale=planes[j][:, P * fb : P * fb + P],
+                    rhs=w_sb[j][:, 2 * f0 : 2 * f0 + 512].bitcast(FP4),
+                    rhs_scale=planes[j][:, f0 : f0 + 256],
                     start=True, stop=True,
                 )
             return da
 
-        def gate_a(k, b, da):
+        def gate_a(k, h, da):
             j, q, g = slot_of(k)
             nc.vector.scalar_tensor_tensor(
-                out=mds[k][:, P * b : P * b + P, :],
-                in0=v_sb[2 * j + g, q][:, :, P * b : P * b + P].rearrange("p t f -> p f t"),
+                out=mds[k][:, h, :, :],
+                in0=v_sb[2 * j + g, q][:, 2 * h : 2 * h + 2, 0:256].rearrange("p t f -> p f t"),
                 scalar=0.0,
                 in1=da[:].rearrange("p t f -> p f t"),
                 op0=ALU.is_ge, op1=ALU.mult,
@@ -235,17 +246,14 @@ def tile_pact_threshold_grad_s14_kernel(tc, e, wt_words, wt_scales, v, beta, c, 
 
         def scale_a(k):
             j, q, g = slot_of(k)
-            n = P * len(a_blocks(k))
-            if n:
+            if a_blocks(k):
+                beta_row = betab[j][:, 512 * q : 512 * q + 256]
                 nc.gpsimd.tensor_tensor(
-                    out=zs[k][:, 0:n, :], in0=mds[k][:, 0:n, :],
-                    in1=betab[j][:, 512 * q : 512 * q + n].unsqueeze(2).to_broadcast([P, n, 4]),
+                    out=zs[k][:, 0:256, :].rearrange("p f (h r) -> p f h r", h=2),
+                    in0=mds[k][:].rearrange("p h f r -> p f h r"),
+                    in1=beta_row.unsqueeze(2).unsqueeze(3).to_broadcast([P, 256, 2, 2]),
                     op=ALU.mult,
                 )
-
-        def hold_gpsimd(k):
-            tick = work.tile([P, 1], U32, name="tick")
-            nc.gpsimd.tensor_copy(out=tick[:], in_=z_codes[k][:, 511:512])
 
         def mm_b(k, b):
             j, q, g = slot_of(k)
@@ -361,65 +369,71 @@ def tile_pact_threshold_grad_s14_kernel(tc, e, wt_words, wt_scales, v, beta, c, 
         e_quant(0)
         for half in range(2):
             et = e_transpose(1, half, "da")
-            e_copy(1, half, et, half == 1)
+            e_copy(1, half, et, half in HEAD_V and half == 1)
         e_quant(1)
 
         for k in range(N_SLOT):
             late, now_a, now_b = y_groups(k - 1), a_blocks(k), b_blocks(k)
             first = sum(SECOND[:k])
             groups = [(i // 4, i % 4) for i in range(first, first + SECOND[k])]
-            open_z(k)
+            open_md(k)
             for group, bank in zip(late, ("yt", "et")):
                 y_transpose(k - 1, group, bank)
             for i, (n, half) in enumerate(E_JOBS.get(k, [])):
                 e_copy(n, half, e_transpose(n, half, "ob" if i else None))
-            if k in (1, 2):
-                beta_rows(k)
-            if k in E_QUANT:
-                e_quant(E_QUANT[k])
-            if k in (3, 4):
-                c_quant(k - 3)
             for i in QUANT.get(k, [k - 3] if k >= 3 else []):
                 z_quant(i)
-                hold_gpsimd(i)
+            if k in E_QUANT:
+                e_quant(E_QUANT[k])
+            for g in range(2):
+                if C_QUANT[g] == k:
+                    c_quant(g)
             if k >= 1:
+                open_z(k - 1)
                 scale_a(k - 1)
             for group in late:
                 gate_b(k - 1, group)
-            for b in now_b[:2]:
-                mm_b(k, b)
+            todo_a, todo_b, todo_s = list(now_a), list(now_b), list(groups)
             obs = []
-            rest = now_a + now_b[2:]
-            for i in range(max(len(rest), len(groups))):
-                if i < len(now_a):
-                    da = mm_a(k, now_a[i])
-                    gate_a(k, now_a[i], da)
-                elif i < len(rest):
-                    mm_b(k, rest[i])
-                if i < len(groups):
-                    obs.append(second(*groups[i]))
-            for i in range(len(groups)):
-                finish(*groups[i], obs[i], False)
-            if k in (0, 2):
-                beta_rows(k + k // 2)
+            for step in ORDER + "BABABABAsss":
+                if step == "A" and todo_a:
+                    b = todo_a[0]
+                    todo_a = todo_a[1:]
+                    gate_a(k, b, mm_a(k, b))
+                if step == "B" and todo_b:
+                    mm_b(k, todo_b[0])
+                    todo_b = todo_b[1:]
+                if step == "s" and todo_s:
+                    obs.append(second(*todo_s[0]))
+                    todo_s = todo_s[1:]
+                    if EARLY:
+                        finish(*groups[len(obs) - 1], obs[-1], False)
+            if not EARLY:
+                for i in range(len(groups)):
+                    finish(*groups[i], obs[i], k == 15 and i in V15)
+            if k < 4:
+                beta_rows(k)
             for g, part, on_vector in C_PARTS.get(k, []):
                 c_copy(g, part, on_vector)
         for i in TAIL_QUANT:
             z_quant(i)
+        open_z(15)
         tail = [(i // 4, i % 4) for i in range(sum(SECOND), 28)]
-        for i, group in enumerate(y_groups(15)):
-            y_transpose(15, group, ("yt", "et")[i])
-            if TAIL_SPLIT and i == 0:
-                for unit in tail:
-                    finish(*unit, second(*unit), False)
-        if not TAIL_SPLIT:
-            for unit in tail:
-                finish(*unit, second(*unit), False)
-        for i, group in enumerate(y_groups(15)):
-            gate_b(15, group)
-            if i < len(y_groups(15)) - 1 or len(y_groups(15)) == 1:
-                z_quant(15, 0, 256)
-        z_quant(15, 256, 512)
+        late = y_groups(15)
+        todo = list(tail)
+        for step in TAIL_PE:
+            if step == "T":
+                y_transpose(15, late[0], ("yt", "et")[len(y_groups(15)) - len(late)])
+                late = late[1:]
+            if step == "s" and todo:
+                finish(*todo[0], second(*todo[0], bank=TAIL_BANK[len(tail) - len(todo)]), len(tail) - len(todo) in TAIL_V)
+                todo = todo[1:]
+            if step == "G":
+                i = GDONE.count(1)
+                gate_b(15, y_groups(15)[i])
+                z_quant(15, 256 * i, 256 * i + 256)
+                GDONE.append(1)
+        GDONE.clear()
         for half in range(2):
             for rt in range(4):
                 cols = (256 * half, 256 * half + 256)

from contextlib import ExitStack

import concourse.mybir as mybir
from concourse.masks import make_identity

G, M, O, F, R = 4, 1024, 512, 1024, 512
FLOPS = 2 * G * M * O * F + 2 * G * M * F * R

F32 = mybir.dt.float32
BF16 = mybir.dt.bfloat16
U32 = mybir.dt.uint32
I32 = mybir.dt.int32
U8 = mybir.dt.uint8
FP8 = mybir.dt.float8_e4m3fn_x4
FP4 = mybir.dt.float4_e2m1fn_x4
ALU = mybir.AluOpType
ACT = mybir.ActivationFunctionType

P = 128
N_SLOT = 16
NB = [2] * 15 + [4]
QUANT = {2: [0], 3: [1], 4: [], 14: [11, 12], 15: [13]}
TAIL_QUANT = [14]
V15 = [0, 1]
TAIL_PE = "TssTGG"
TAIL_BANK = ["da", "db"]
TAIL_V = []
GDONE = []
ORDER = "BABAss"
EARLY = False
HEAD_V = [0, 1]
C_QUANT = [4, 4]
E_JOBS = {1: [(2, 0), (2, 1)], 2: [(3, 0)], 3: [(3, 1)], 4: [(4, 0), (4, 1)], 6: [(5, 0), (5, 1)], 8: [(6, 0), (6, 1)], 10: [(7, 0), (7, 1)]}
E_QUANT = {2: 2, 4: 3, 6: 4, 8: 5, 10: 6, 12: 7}
C_PARTS = {1: [(0, 3, 0), (0, 0, 0)], 2: [(1, 3, 1), (0, 1, 0)], 3: [(1, 2, 1), (0, 2, 0), (1, 1, 0), (1, 0, 0)]}
SECOND = [0] * 4 + [2] * 10 + [3, 3]


def tile_pact_threshold_grad_s14_kernel(tc, e, wt_words, wt_scales, v, beta, c, out):
    nc = tc.nc
    with ExitStack() as ctx:
        keep = ctx.enter_context(tc.tile_pool(name="keep", bufs=1))
        work = ctx.enter_context(tc.tile_pool(name="work", bufs=2))
        psum = ctx.enter_context(tc.psum_pool(name="psum", bufs=2))
        ctx.enter_context(tc.manual_schedule())

        def slot_of(k):
            return k // 4, (k % 4) // 2, k % 2

        planes = {}
        planes[0] = keep.tile([P, F], U8, align_bytes=64, name="planes0")
        plane_rest = keep.tile([P, 3 * F], U8, align_bytes=64, name="plane_rest")
        for j in range(1, G):
            planes[j] = plane_rest[:, F * (j - 1) : F * j]
        nc.vector.memset(planes[0][:].bitcast(I32), 0)
        brow = keep.tile([P, P], BF16, align_bytes=64, name="brow")
        nc.vector.memset(brow[:], 0.0)
        warm = keep.tile([P, 2], F32, name="warm")
        nc.vector.memset(warm[:], 0.0)
        nc.vector.memset(plane_rest[:].bitcast(I32), 0)
        w_sb = {}
        for j in range(G):
            w_sb[j] = keep.tile([P, 2 * F], U8, align_bytes=64, name="w_sb%d" % j)
        nc.gpsimd.dma_start(out=w_sb[0][:].bitcast(I32), in_=wt_words[0].bitcast(I32))
        nc.gpsimd.dma_start(out=brow[0:32, :], in_=beta.rearrange("j (b f) -> (j b) f", f=P))
        ident_f = keep.tile([P, P], F32, align_bytes=64, name="ident_f")
        make_identity(nc, ident_f[:])
        ident_b = keep.tile([P, P], BF16, align_bytes=64, name="ident_b")
        make_identity(nc, ident_b[:])

        nc.scalar.activation(out=warm[:, 1:2], in_=warm[:, 0:1], func=ACT.Copy, scale=1.0)

        e_sb, v_sb, e_codes, e_scales, betab = {}, {}, {}, {}, {}
        for n in range(8):
            e_sb[n] = keep.tile([P, 4 * O], BF16, align_bytes=64, name="e_sb%d" % n)
            if n < 2:
                for q in range(2):
                    v_sb[n, q] = keep.tile([P, 4, 512], BF16, align_bytes=64, name="v_sb%d_%d" % (n, q))
            else:
                v_full = keep.tile([P, 4, F], BF16, align_bytes=64, name="v_sb%d" % n)
                v_sb[n] = v_full
                for q in range(2):
                    v_sb[n, q] = v_full[:, :, 512 * q : 512 * q + 512]
            e_codes[n] = keep.tile([P, 512], U32, align_bytes=64, name="e_codes%d" % n)
            e_scales[n] = keep.tile([P, 512], U8, align_bytes=64, name="e_scales%d" % n)
        for j in range(G):
            betab[j] = keep.tile([P, F], BF16, align_bytes=64, name="betab%d" % j)
        c_sb = keep.tile([P, 2, 4, R], BF16, align_bytes=64, name="c_sb")

        def load_e(n, half=None):
            j, g = n // 2, n % 2
            rows = slice(0, 4) if half is None else slice(2 * half, 2 * half + 2)
            nc.sync.dma_start(
                out=e_sb[n][:].rearrange("p (t k) -> p t k", t=4)[:, rows, :],
                in_=e[j, 512 * g : 512 * g + 512, :].rearrange("(p t) k -> p t k", t=4)[:, rows, :],
            )

        def load_v(n, q=None):
            j, g = n // 2, n % 2
            rows = v[j, 512 * g : 512 * g + 512, :].rearrange("(p t) f -> p t f", t=4)
            if q is None:
                nc.sync.dma_start(out=v_sb[n][:], in_=rows)
            else:
                nc.sync.dma_start(out=v_sb[n, q][:], in_=rows[:, :, 512 * q : 512 * q + 512])

        def load_w(j):
            nc.sync.dma_start(out=w_sb[j][:].bitcast(I32), in_=wt_words[j].bitcast(I32))

        def load_c(g):
            nc.sync.dma_start(
                out=c_sb[:, g, :, :],
                in_=c[512 * g : 512 * g + 512, :].rearrange("(p t) r -> p t r", t=4),
            )

        def load_planes_first():
            for quad in range(4):
                nc.sync.dma_start(
                    out=planes[0][32 * quad : 32 * quad + 4, :].bitcast(I32),
                    in_=wt_scales[0, 4 * quad : 4 * quad + 4, :].bitcast(I32),
                )

        def load_planes_rest():
            for quad in range(4):
                nc.sync.dma_start(
                    out=plane_rest[32 * quad : 32 * quad + 4, :].bitcast(I32).rearrange("r (j n) -> r j n", j=3),
                    in_=wt_scales[1:4, 4 * quad : 4 * quad + 4, :].bitcast(I32).rearrange("j r n -> r j n"),
                )

        load_e(0, 0)
        load_e(0, 1)
        load_planes_first()
        load_e(1)
        load_v(0, 0)
        load_v(1, 0)
        load_e(2)
        load_v(0, 1)
        load_c(0)
        load_e(3)
        load_v(1, 1)
        load_c(1)
        load_e(4)
        for j in range(1, G):
            load_w(j)
            if j == 1:
                load_planes_rest()
            load_v(2 * j)
            for n in (2 * j + 3, 2 * j + 4):
                if n < 2 * G:
                    load_e(n)
            load_v(2 * j + 1)

        e_grp = {}

        def e_transpose(n, half, tag=None):
            if half == 0:
                eg = work.tile([P, 2048], BF16, align_bytes=64, name="eg")
                e_grp[n] = eg
            if tag == "ob":
                et = psum.tile([P, 2, 2, P], F32, name="ob")
            elif tag == "da":
                et = psum.tile([P, 2, 2, P], F32, name="da")
            else:
                et = psum.tile([P, 2, 2, P], F32, bufs=1, name="et")
            words = e_sb[n][:].bitcast(F32)
            for tt in range(2):
                for u in range(2):
                    lo = 256 * (2 * half + tt)
                    nc.tensor.transpose(et[:, tt, u, :], words[:, lo + u : lo + 256 : 2], ident_f[:])
            return et

        def e_copy(n, half, et, on_vector=False):
            dst = e_grp[n][:, 1024 * half : 1024 * half + 1024].bitcast(F32)
            dst = dst.rearrange("p (t m u) -> p t m u", t=2, u=2)
            src = et[:].rearrange("p t u m -> p t m u")
            if on_vector:
                nc.vector.tensor_copy(out=dst, in_=src)
            else:
                nc.scalar.copy(out=dst, in_=src)

        def e_quant(n):
            nc.vector.quantize_mx(out=e_codes[n][:].bitcast(FP8), scales=e_scales[n][:], in_=e_grp[n][:])

        def a_blocks(k):
            return list(range(4 - NB[k])) if 0 <= k < N_SLOT else []

        def b_blocks(k):
            return list(range(4 - NB[k], 4)) if 0 <= k < N_SLOT else []

        bcol_b = keep.tile([P, 32], BF16, name="bcol_b")
        bcol_f = keep.tile([P, 32], F32, name="bcol_f")

        def beta_columns():
            yt = psum.tile([P, 4, 2 * P], BF16, bufs=1, name="yt")
            nc.tensor.transpose(yt[:, 0, 0:P], brow[:], ident_b[:])
            nc.scalar.copy(out=bcol_b[:], in_=yt[:, 0, 0:32])
            nc.vector.tensor_copy(out=bcol_f[:], in_=yt[:, 0, 0:32])

        def beta_rows(j):
            bt = psum.tile([P, 2, 4, P], BF16, name="ob")
            count = max(len(a_blocks(k)) for k in range(4 * j, 4 * j + 4))
            for q in range(2):
                for b in range(count):
                    i = 8 * j + 4 * q + b
                    nc.tensor.transpose(bt[:, q, b, :], bcol_b[:, i : i + 1].to_broadcast([P, P]), ident_b[:])
            nc.scalar.copy(
                out=betab[j][:].rearrange("p (q b f) -> p q b f", q=2, b=4)[:, :, 0:count, :],
                in_=bt[:, :, 0:count, :],
            )

        mds, zs, ys, yts = {}, {}, {}, {}

        def open_z(k):
            z = work.tile([P, 512, 4], BF16, align_bytes=64, name="z")
            zs[k] = z

        def open_md(k):
            if a_blocks(k):
                md = work.tile([P, 2, 256, 2], F32, align_bytes=64, bufs=3, name="md")
                mds[k] = md

        def mm_a(k, h):
            j, q, g = slot_of(k)
            n, f0 = 2 * j + g, 512 * q
            da = psum.tile([P, 2, 2 * P], F32, name="da")
            for r in range(2):
                t = 2 * h + r
                cols = slice(P * t, P * t + P)
                nc.tensor.matmul_mx(
                    out=da[:, r, :],
                    lhsT=e_codes[n][:, cols].bitcast(FP8), lhsT_scale=e_scales[n][:, cols],
                    rhs=w_sb[j][:, 2 * f0 : 2 * f0 + 512].bitcast(FP4),
                    rhs_scale=planes[j][:, f0 : f0 + 256],
                    start=True, stop=True,
                )
            return da

        def gate_a(k, h, da):
            j, q, g = slot_of(k)
            nc.vector.scalar_tensor_tensor(
                out=mds[k][:, h, :, :],
                in0=v_sb[2 * j + g, q][:, 2 * h : 2 * h + 2, 0:256].rearrange("p t f -> p f t"),
                scalar=0.0,
                in1=da[:].rearrange("p t f -> p f t"),
                op0=ALU.is_ge, op1=ALU.mult,
            )

        def scale_a(k):
            j, q, g = slot_of(k)
            if a_blocks(k):
                beta_row = betab[j][:, 512 * q : 512 * q + 256]
                nc.gpsimd.tensor_tensor(
                    out=zs[k][:, 0:256, :].rearrange("p f (h r) -> p f h r", h=2),
                    in0=mds[k][:].rearrange("p h f r -> p f h r"),
                    in1=beta_row.unsqueeze(2).unsqueeze(3).to_broadcast([P, 256, 2, 2]),
                    op=ALU.mult,
                )

        def mm_b(k, b):
            j, q, g = slot_of(k)
            n, fb = 2 * j + g, 4 * q + b
            if b_blocks(k).index(b) < 2:
                db = psum.tile([P, 512], F32, name="db")
            else:
                db = psum.tile([P, 512], F32, name="da")
            nc.tensor.matmul_mx(
                out=db[:],
                lhsT=w_sb[j][:, 256 * fb : 256 * fb + 256].bitcast(FP4),
                lhsT_scale=planes[j][:, P * fb : P * fb + P],
                rhs=e_codes[n][:].bitcast(FP8), rhs_scale=e_scales[n][:],
                start=True, stop=True,
            )
            y = work.tile([P, 512], BF16, align_bytes=64, bufs=4, name="y")
            i = 8 * j + fb
            nc.scalar.activation(out=y[:], in_=db[:], func=ACT.Copy, scale=bcol_f[:, i : i + 1])
            ys[k, b] = y

        def y_groups(k):
            blocks = b_blocks(k)
            return [blocks[i : i + 2] for i in range(0, len(blocks), 2)]

        def y_transpose(k, group, bank="yt"):
            if bank == "yt":
                yt = psum.tile([P, 4, 2 * P], BF16, bufs=1, name="yt")
            else:
                yt = psum.tile([P, 4, 2 * P], BF16, bufs=1, name="et")
            for i, b in enumerate(group):
                for t in range(4):
                    nc.tensor.transpose(
                        yt[:, t, P * i : P * i + P], ys[k, b][:, P * t : P * t + P], ident_b[:]
                    )
            yts[k, group[0]] = yt

        def gate_b(k, group):
            j, q, g = slot_of(k)
            n = P * len(group)
            cols = slice(P * group[0], P * group[0] + n)
            nc.vector.scalar_tensor_tensor(
                out=zs[k][:, cols, :],
                in0=v_sb[2 * j + g, q][:, :, cols].rearrange("p t f -> p f t"),
                scalar=0.0,
                in1=yts[k, group[0]][:, :, 0:n].rearrange("p t f -> p f t"),
                op0=ALU.is_ge, op1=ALU.mult,
            )

        z_codes, z_scales = {}, {}

        def z_quant(k, lo=0, hi=512):
            if lo == 0:
                zc = work.tile([P, 512], U32, align_bytes=64, bufs=5, name="zc")
                zp = work.tile([P, 512], U8, align_bytes=64, bufs=5, name="zp")
                z_codes[k], z_scales[k] = zc, zp
            nc.vector.quantize_mx(
                out=z_codes[k][:, lo:hi].bitcast(FP8), scales=z_scales[k][:, lo:hi],
                in_=zs[k][:, lo:hi, :].rearrange("p f t -> p (f t)"),
            )

        c_codes = keep.tile([P, 2 * R], U32, align_bytes=64, name="c_codes")
        c_scales = keep.tile([P, 2 * R], U8, align_bytes=64, name="c_scales")
        c_grp = keep.tile([P, 2, R, 4], BF16, align_bytes=64, name="c_grp")

        def c_copy(g, part, on_vector):
            cols = slice(128 * part, 128 * part + 128)
            dst, src = c_grp[:, g, cols, :], c_sb[:, g, :, cols].rearrange("p t r -> p r t")
            if on_vector:
                nc.vector.tensor_copy(out=dst, in_=src)
            else:
                nc.scalar.copy(out=dst, in_=src)

        def c_quant(g):
            cols = slice(R * g, R * g + R)
            nc.vector.quantize_mx(
                out=c_codes[:, cols].bitcast(FP8), scales=c_scales[:, cols],
                in_=c_grp[:, g, :, :].rearrange("p r t -> p (r t)"),
            )

        def second(pair, rt, lo=0, hi=512, bank="ob"):
            if bank == "ob":
                ob = psum.tile([P, 512], F32, name="ob")
            elif bank == "da":
                ob = psum.tile([P, 512], F32, name="da")
            else:
                ob = psum.tile([P, 512], F32, name="db")
            for g in range(2):
                k = 2 * pair + g
                cols = slice(R * g + P * rt, R * g + P * rt + P)
                nc.tensor.matmul_mx(
                    out=ob[:, lo:hi],
                    lhsT=c_codes[:, cols].bitcast(FP8), lhsT_scale=c_scales[:, cols],
                    rhs=z_codes[k][:, lo:hi].bitcast(FP8), rhs_scale=z_scales[k][:, lo:hi],
                    start=(g == 0), stop=(g == 1),
                )
            return ob

        def finish(pair, rt, ob, on_vector, lo=0, hi=512):
            j, q = pair // 2, pair % 2
            ot = work.tile([P, 512], F32, bufs=10, name="ot")
            if on_vector:
                nc.vector.tensor_copy(out=ot[:, lo:hi], in_=ob[:, lo:hi])
            else:
                nc.scalar.copy(out=ot[:, lo:hi], in_=ob[:, lo:hi])
            nc.sync.dma_start(
                out=out[j, P * rt : P * rt + P, 512 * q + lo : 512 * q + hi], in_=ot[:, lo:hi]
            )

        for half in range(2):
            et = e_transpose(0, half, "ob")
            e_copy(0, half, et, half == 1)
        beta_columns()
        e_quant(0)
        for half in range(2):
            et = e_transpose(1, half, "da")
            e_copy(1, half, et, half in HEAD_V and half == 1)
        e_quant(1)

        for k in range(N_SLOT):
            late, now_a, now_b = y_groups(k - 1), a_blocks(k), b_blocks(k)
            first = sum(SECOND[:k])
            groups = [(i // 4, i % 4) for i in range(first, first + SECOND[k])]
            open_md(k)
            for group, bank in zip(late, ("yt", "et")):
                y_transpose(k - 1, group, bank)
            for i, (n, half) in enumerate(E_JOBS.get(k, [])):
                e_copy(n, half, e_transpose(n, half, "ob" if i else None))
            for i in QUANT.get(k, [k - 3] if k >= 3 else []):
                z_quant(i)
            if k in E_QUANT:
                e_quant(E_QUANT[k])
            for g in range(2):
                if C_QUANT[g] == k:
                    c_quant(g)
            if k >= 1:
                open_z(k - 1)
                scale_a(k - 1)
            for group in late:
                gate_b(k - 1, group)
            todo_a, todo_b, todo_s = list(now_a), list(now_b), list(groups)
            obs = []
            for step in ORDER + "BABABABAsss":
                if step == "A" and todo_a:
                    b = todo_a[0]
                    todo_a = todo_a[1:]
                    gate_a(k, b, mm_a(k, b))
                if step == "B" and todo_b:
                    mm_b(k, todo_b[0])
                    todo_b = todo_b[1:]
                if step == "s" and todo_s:
                    obs.append(second(*todo_s[0]))
                    todo_s = todo_s[1:]
                    if EARLY:
                        finish(*groups[len(obs) - 1], obs[-1], False)
            if not EARLY:
                for i in range(len(groups)):
                    finish(*groups[i], obs[i], k == 15 and i in V15)
            if k < 4:
                beta_rows(k)
            for g, part, on_vector in C_PARTS.get(k, []):
                c_copy(g, part, on_vector)
        for i in TAIL_QUANT:
            z_quant(i)
        open_z(15)
        tail = [(i // 4, i % 4) for i in range(sum(SECOND), 28)]
        late = y_groups(15)
        todo = list(tail)
        for step in TAIL_PE:
            if step == "T":
                y_transpose(15, late[0], ("yt", "et")[len(y_groups(15)) - len(late)])
                late = late[1:]
            if step == "s" and todo:
                finish(*todo[0], second(*todo[0], bank=TAIL_BANK[len(tail) - len(todo)]), len(tail) - len(todo) in TAIL_V)
                todo = todo[1:]
            if step == "G":
                i = GDONE.count(1)
                gate_b(15, y_groups(15)[i])
                z_quant(15, 256 * i, 256 * i + 256)
                GDONE.append(1)
        GDONE.clear()
        for half in range(2):
            for rt in range(4):
                cols = (256 * half, 256 * half + 256)
                bank = ("ob", "da", "ob", "db")[rt]
                finish(7, rt, second(7, rt, *cols, bank), rt % 2 == 1, *cols)
